import numpy as np
import ml_dtypes


def mxq(x, axis, fmt="e4m3"):
    dtype, down = {"e4m3": (ml_dtypes.float8_e4m3fn, 7), "e5m2": (ml_dtypes.float8_e5m2, 14)}[fmt]
    v = np.moveaxis(np.asarray(x, np.float32).astype(ml_dtypes.bfloat16).astype(np.float64), axis, -1)
    blocks = v.reshape(v.shape[:-1] + (-1, 32))
    amax = np.abs(blocks).max(-1, keepdims=True)
    byte = np.maximum(np.where(amax > 0, np.frexp(amax)[1] - 1 + 127, 0) - down, 1)
    scale = np.exp2(byte - 127.0)
    codes = (blocks / scale).astype(np.float32).astype(dtype).astype(np.float64)
    return np.moveaxis((codes * scale).reshape(v.shape), -1, axis)


WIDE = False


def mx_kscale(k):
    if not WIDE:
        return np.ones(k)
    levels = np.array([10, -10, 5, -5, 0])
    if k % 512:
        return np.exp2(np.random.permutation(np.resize(levels, k // 32))).repeat(32)
    a = np.empty((k // 512, 16))
    for p in range(k // 512):
        a[p, :8] = np.random.permutation(np.resize(levels, 8))
        for g in range(8):
            far = levels[np.abs(levels - a[p, g]) >= 10]
            a[p, g + 8] = far[np.random.randint(len(far))]
    return np.exp2(a.ravel()).repeat(32)


def f64(x):
    return np.asarray(x).astype(np.float64)


def striped8(idx):
    return np.asarray(idx).reshape(8, -1, 16).transpose(0, 2, 1).reshape(128, -1).astype(np.uint16)


def unstriped8(offs):
    return offs.reshape(8, 16, -1).transpose(0, 2, 1).reshape(8, -1).astype(np.int64)


def pick8(x, idx, run):
    r = np.arange(len(x))
    return x[r[:, None], idx[r % (8 * run) // run]]


E2M1 = np.array([0.0, 0.5, 1.0, 1.5, 2.0, 3.0, 4.0, 6.0, -0.0, -0.5, -1.0, -1.5, -2.0, -3.0, -4.0, -6.0])


def pack_weight(w, fmt):
    k, n = w.shape
    w = f64(np.asarray(w, np.float32).astype(ml_dtypes.bfloat16)).reshape(k // 32, 32, n)
    amax = np.abs(w).max(1)
    if fmt == "e4m3":
        byte = np.frexp(amax)[1] - 1 + 127 - 7
    else:
        mant, ex = np.frexp(amax / 6.0)
        byte = np.where(mant > 0.5, ex, ex - 1) + 127
    byte = np.clip(np.where(amax > 0, byte, 1), 1, 254)
    scaled = (w * np.exp2(127.0 - byte)[:, None, :]).reshape(k, n).astype(np.float32)
    by_word = np.ascontiguousarray(scaled.reshape(k // 512, 128, 4, n).transpose(0, 1, 3, 2))
    if fmt == "e4m3":
        words = by_word.astype(ml_dtypes.float8_e4m3fn).view(np.uint8)
    else:
        c = by_word.astype(ml_dtypes.float4_e2m1fn).view(np.uint8) & 0xF
        words = (c[..., 0::2] | (c[..., 1::2] << 4)).reshape(k // 512, 128, 2 * n)
    return np.ascontiguousarray(words), np.ascontiguousarray(byte.astype(np.uint8).reshape(k // 512, 16, n))


def unpack_weight(words, scales, fmt):
    g, _, n = scales.shape
    words = np.ascontiguousarray(words).reshape(g, 128, n, -1)
    if fmt == "e4m3":
        vals = words.view(ml_dtypes.float8_e4m3fn).astype(np.float64)
    else:
        nib = np.empty((g, 128, n, 4), np.uint8)
        nib[..., 0::2] = words & 0xF
        nib[..., 1::2] = words >> 4
        vals = E2M1[nib]
    vals = vals * np.repeat(np.exp2(scales.astype(np.float64) - 127.0), 8, axis=1)[..., None]
    return vals.transpose(0, 1, 3, 2).reshape(g * 512, n)


def sgn(shape):
    return np.random.uniform(0.5, 2.0, shape) * np.where(np.random.standard_normal(shape) < 0, -1.0, 1.0)


D, T, U, X, I, Q = 512, 1024, 1024, 1024, 512, 128


def setup_inputs():
    n = np.random.standard_normal
    idx = np.stack([np.random.permutation(T)[:I] for _ in range(8)])
    idx2 = np.stack([np.random.permutation(U)[:I] for _ in range(8)])
    idx3 = np.stack([np.random.permutation(X)[:I] for _ in range(8)])
    idx4 = np.stack([np.random.permutation(U)[:I] for _ in range(8)])
    idx5 = np.stack([np.random.permutation(U)[:I] for _ in range(8)])
    idx6 = np.stack([np.random.permutation(X)[:I] for _ in range(8)])
    fd = mx_kscale(D)
    cachep = pack_weight(n((D, T)) / fd[:, None], "e2m1")
    draftp = pack_weight(n((D, U)) / fd[:, None], "e4m3")
    archp = pack_weight(n((D, X)) / fd[:, None], "e2m1")
    return {
        "query": (n((D, Q)) * 1.0 / np.sqrt(D) * fd[:, None]).astype(np.float32),
        "cache_words": cachep[0],
        "cache_scales": cachep[1],
        "draft_words": draftp[0],
        "draft_scales": draftp[1],
        "arch_words": archp[0],
        "arch_scales": archp[1],
        "sa": (sgn((Q, 1))).astype(np.float32),
        "sb": (sgn((Q, 1))).astype(np.float32),
        "offs": striped8(idx),
        "offs2": striped8(idx2),
        "offs3": striped8(idx3),
        "offs4": striped8(idx4),
        "offs5": striped8(idx5),
        "offs6": striped8(idx6),
    }


def reference(query, cache_words, cache_scales, draft_words, draft_scales, arch_words, arch_scales, sa, sb, offs, offs2, offs3, offs4, offs5, offs6):
    idx = unstriped8(offs)
    idx2 = unstriped8(offs2)
    idx3 = unstriped8(offs3)
    idx4 = unstriped8(offs4)
    idx5 = unstriped8(offs5)
    idx6 = unstriped8(offs6)
    cacheu = unpack_weight(cache_words, cache_scales, "e2m1")
    draftu = unpack_weight(draft_words, draft_scales, "e4m3")
    archu = unpack_weight(arch_words, arch_scales, "e2m1")
    queryq = mxq(f64(query), 0, "e4m3")
    a = queryq.T @ cacheu
    b = queryq.T @ draftu
    c0 = queryq.T @ archu
    w = pick8(a, idx, 16) * f64(sa)
    v = pick8(b, idx2, 16) * f64(sb)
    r = w - v
    f1 = np.zeros((Q, X))
    f1[np.arange(Q)[:, None], idx3[np.arange(Q) % 128 // 16]] = r
    cc = c0 - f1
    f2 = np.zeros((Q, U))
    f2[np.arange(Q)[:, None], idx4[np.arange(Q) % 128 // 16]] = w
    bb = np.maximum(b, f2)
    y = pick8(bb, idx5, 16) - pick8(cc, idx6, 16)
    return y

@@ -1,0 +1,151 @@
+from contextlib import ExitStack
+
+import concourse.mybir as mybir
+
+F32 = mybir.dt.float32
+BF16 = mybir.dt.bfloat16
+I32 = mybir.dt.int32
+U32 = mybir.dt.uint32
+U16 = mybir.dt.uint16
+U8 = mybir.dt.uint8
+FP8X4 = mybir.dt.float8_e4m3fn_x4
+FP4X4 = mybir.dt.float4_e2m1fn_x4
+COPY = mybir.ActivationFunctionType.Copy
+SUB = mybir.AluOpType.subtract
+MAX = mybir.AluOpType.max
+
+P = 128
+PACK = 4
+Q = 128
+TOK = 1024
+SLOTS = 512
+HALF = SLOTS // 2
+BANK = 512
+FLOPS = 3 * 2 * 512 * Q * TOK
+
+
+def tile_attend_scaledlead_three_kernel(tc, query, cache_words, cache_scales, draft_words, draft_scales,
+                                         arch_words, arch_scales, sa, sb, offs, offs2, offs3, offs4, offs5,
+                                         offs6, out):
+    nc = tc.nc
+    with ExitStack() as ctx:
+        keep = ctx.enter_context(tc.tile_pool(name="keep", bufs=1))
+        psum = ctx.enter_context(tc.psum_pool(name="psum", bufs=1))
+
+        def load_list(src, name):
+            t = keep.tile([P, SLOTS // 16], U16, name=name)
+            nc.sync.dma_start(t[:], src)
+            return t
+
+        def plane(name):
+            t = keep.tile([P, TOK], U8, name=name, align_bytes=64)
+            nc.vector.memset(t[:].bitcast(I32), 0)
+            return t
+
+        def load_scales(queue, t, src, g):
+            queue.dma_start(t[32 * g:32 * g + 4, :].bitcast(I32), src[0, 4 * g:4 * g + 4, :].bitcast(I32))
+
+        cache_s = plane("cache_s")
+        draft_s = plane("draft_s")
+        arch_s = plane("arch_s")
+        q_raw = keep.tile([P, PACK, Q], F32, name="q_raw")
+        cache_w = keep.tile([P, 2 * TOK], U8, name="cache_w", align_bytes=64)
+        draft_w = keep.tile([P, TOK], I32, name="draft_w", align_bytes=64)
+        arch_w = keep.tile([P, 2 * TOK], U8, name="arch_w", align_bytes=64)
+        sa_t = keep.tile([P, 1], F32, name="sa_t")
+        sb_t = keep.tile([P, 1], F32, name="sb_t")
+        nc.sync.dma_start(q_raw[:], query.rearrange("(p j) q -> p j q", j=PACK))
+        load_scales(nc.sync, cache_s, cache_scales, 0)
+        load_scales(nc.sync, cache_s, cache_scales, 1)
+        load_scales(nc.sync, cache_s, cache_scales, 2)
+        load_scales(nc.sync, cache_s, cache_scales, 3)
+        nc.sync.dma_start(cache_w[:].bitcast(I32), cache_words[0].bitcast(I32))
+        nc.sync.dma_start(draft_w[:], draft_words[0].rearrange("p n t -> p (n t)").bitcast(I32))
+        load_scales(nc.sync, draft_s, draft_scales, 0)
+        load_scales(nc.sync, draft_s, draft_scales, 1)
+        load_scales(nc.sync, draft_s, draft_scales, 2)
+        load_scales(nc.sync, draft_s, draft_scales, 3)
+        list1 = load_list(offs, "list1")
+        nc.sync.dma_start(sa_t[:], sa)
+        list2 = load_list(offs2, "list2")
+        nc.sync.dma_start(sb_t[:], sb)
+        list3 = load_list(offs3, "list3")
+        list4 = load_list(offs4, "list4")
+        nc.sync.dma_start(arch_w[:].bitcast(I32), arch_words[0].bitcast(I32))
+        load_scales(nc.sync, arch_s, arch_scales, 0)
+        load_scales(nc.sync, arch_s, arch_scales, 1)
+        load_scales(nc.sync, arch_s, arch_scales, 2)
+        load_scales(nc.sync, arch_s, arch_scales, 3)
+        list6 = load_list(offs6, "list6")
+        list5 = load_list(offs5, "list5")
+
+        q_bf = keep.tile([P, Q, PACK], BF16, name="q_bf", align_bytes=64)
+        q_w = keep.tile([P, Q], U32, name="q_w", align_bytes=64)
+        q_s = keep.tile([P, Q], U8, name="q_s", align_bytes=64)
+        q_halves = [slice(0, Q // 2), slice(Q // 2, Q)]
+        for qs in q_halves:
+            nc.vector.tensor_copy(q_bf[:, qs, :].rearrange("p (c i) t -> p c t i", i=4),
+                                  q_raw[:, :, qs].rearrange("p t (c i) -> p c t i", i=4))
+        for qs in q_halves:
+            nc.vector.quantize_mx(out=q_w[:, qs].bitcast(FP8X4), scales=q_s[:, qs],
+                                  in_=q_bf[:, qs, :].rearrange("p c t -> p (c t)"))
+
+        def scores(name, tag, c0, c1, rhs, rhs_scale):
+            bank = psum.tile([P, c1 - c0], F32, name=name, tag=tag)
+            nc.tensor.matmul_mx(out=bank[:], lhsT=q_w[:].bitcast(FP8X4), lhsT_scale=q_s[:],
+                                rhs=rhs, rhs_scale=rhs_scale[:, c0:c1], start=True, stop=True)
+            return bank
+
+        a = keep.tile([P, TOK], F32, name="a", tag="a_f1")
+        for n, (c0, c1) in enumerate(((0, 512), (512, 768), (768, 896), (896, 1024))):
+            bank = scores("a%d" % n, "a%d" % n, c0, c1, cache_w[:, 2 * c0:2 * c1].bitcast(FP4X4), cache_s)
+            if n % 2 == 0:
+                nc.scalar.copy(a[:, c0:c1], bank[:])
+            else:
+                nc.vector.tensor_copy(a[:, c0:c1], bank[:])
+
+        b = keep.tile([P, TOK], F32, name="b")
+        for n, c0 in enumerate(range(0, TOK, 256)):
+            c1 = c0 + 256
+            bank = scores("b%d" % n, "b%d" % n, c0, c1, draft_w[:, c0:c1].bitcast(FP8X4), draft_s)
+            nc.vector.tensor_copy(b[:, c0:c1], bank[:])
+
+        w = keep.tile([P, SLOTS], F32, name="w")
+        nc.scalar.activation(w[:], a[:].indirect(list1[:]), COPY, scale=sa_t[:])
+
+        f1 = [keep.tile([P, TOK], F32, name="f1_0"), keep.tile([P, TOK], F32, name="f1_1", tag="a_f1")]
+        nc.vector.memset(f1[0][:], 0.0)
+        nc.gpsimd.memset(f1[1][:], 0.0)
+
+        halves = [(h, slice(h * HALF, (h + 1) * HALF), slice(h * HALF // 16, (h + 1) * HALF // 16)) for h in range(2)]
+        v = keep.tile([P, SLOTS], F32, name="v", tag="v_f2")
+        r = [keep.tile([P, HALF], F32, name="r%d" % h) for h in range(2)]
+        for h, slots, cols in halves:
+            nc.scalar.activation(v[:, slots], b[:].indirect(list2[:, cols]), COPY, scale=sb_t[:])
+            nc.vector.tensor_tensor(r[h][:], w[:, slots], v[:, slots], SUB)
+        for h, slots, cols in halves:
+            nc.scalar.activation(f1[h][:].indirect(list3[:, cols]), r[h][:], COPY)
+        f2 = keep.tile([P, TOK], F32, name="f2", tag="v_f2")
+        nc.gpsimd.memset(f2[:], 0.0)
+        nc.scalar.activation(f2[:].indirect(list4[:]), w[:], COPY)
+
+        part = keep.tile([P, TOK], F32, name="part")
+        for n, c0 in enumerate(range(0, TOK, BANK)):
+            c1 = c0 + BANK
+            bank = scores("c%d" % n, "a%d" % n, c0, c1, arch_w[:, 2 * c0:2 * c1].bitcast(FP4X4), arch_s)
+            nc.vector.tensor_tensor(part[:, c0:c1], bank[:], f1[0][:, c0:c1], SUB)
+        cc = keep.tile([P, TOK], F32, name="cc", tag="cc_bb")
+        nc.vector.tensor_tensor(cc[:], part[:], f1[1][:], SUB)
+        left = keep.tile([P, SLOTS], F32, name="left")
+        nc.vector.tensor_copy(left[:], cc[:].indirect(list6[:]))
+
+        bb = keep.tile([P, TOK], F32, name="bb", tag="cc_bb")
+        nc.vector.tensor_tensor(bb[:], b[:], f2[:], MAX)
+        y = [keep.tile([P, HALF], F32, name="y%d" % h) for h in range(2)]
+        picked = keep.tile([P, HALF], F32, name="picked")
+        (h0, slots0, cols0), (h1, slots1, cols1) = halves
+        nc.scalar.activation(picked[:], bb[:].indirect(list5[:, cols1]), COPY)
+        nc.vector.tensor_tensor(y[0][:], bb[:].indirect(list5[:, cols0]), left[:, slots0], SUB)
+        nc.sync.dma_start(out[:, slots0], y[0][:])
+        nc.vector.tensor_tensor(y[1][:], picked[:], left[:, slots1], SUB)
+        nc.scalar.dma_start(out[:, slots1], y[1][:])

@@ -49,28 +49,28 @@ def tile_attend_scaledlead_three_kernel(tc, query, cache_words, cache_scales, dr
         draft_s = plane("draft_s")
         arch_s = plane("arch_s")
         q_raw = keep.tile([P, PACK, Q], F32, name="q_raw")
-        cache_w = keep.tile([P, 2 * TOK], U8, name="cache_w", align_bytes=64)
+        cache_w = keep.tile([P, 2 * TOK], U8, name="cache_w", tag="cw_f1", align_bytes=64)
         draft_w = keep.tile([P, TOK], I32, name="draft_w", align_bytes=64)
         arch_w = keep.tile([P, 2 * TOK], U8, name="arch_w", align_bytes=64)
         sa_t = keep.tile([P, 1], F32, name="sa_t")
         sb_t = keep.tile([P, 1], F32, name="sb_t")
         nc.sync.dma_start(q_raw[:], query.rearrange("(p j) q -> p j q", j=PACK))
+        nc.sync.dma_start(cache_w[:].bitcast(I32), cache_words[0].bitcast(I32))
         load_scales(nc.sync, cache_s, cache_scales, 0)
         load_scales(nc.sync, cache_s, cache_scales, 1)
         load_scales(nc.sync, cache_s, cache_scales, 2)
         load_scales(nc.sync, cache_s, cache_scales, 3)
-        nc.sync.dma_start(cache_w[:].bitcast(I32), cache_words[0].bitcast(I32))
+        nc.sync.dma_start(sa_t[:], sa)
         nc.sync.dma_start(draft_w[:], draft_words[0].rearrange("p n t -> p (n t)").bitcast(I32))
+        list1 = load_list(offs, "list1")
         load_scales(nc.sync, draft_s, draft_scales, 0)
         load_scales(nc.sync, draft_s, draft_scales, 1)
         load_scales(nc.sync, draft_s, draft_scales, 2)
         load_scales(nc.sync, draft_s, draft_scales, 3)
-        list1 = load_list(offs, "list1")
-        nc.sync.dma_start(sa_t[:], sa)
+        list4 = load_list(offs4, "list4")
         list2 = load_list(offs2, "list2")
         nc.sync.dma_start(sb_t[:], sb)
         list3 = load_list(offs3, "list3")
-        list4 = load_list(offs4, "list4")
         nc.sync.dma_start(arch_w[:].bitcast(I32), arch_words[0].bitcast(I32))
         load_scales(nc.sync, arch_s, arch_scales, 0)
         load_scales(nc.sync, arch_s, arch_scales, 1)
@@ -110,40 +110,45 @@ def tile_attend_scaledlead_three_kernel(tc, query, cache_words, cache_scales, dr
             bank = scores("b%d" % n, "b%d" % n, c0, c1, draft_w[:, c0:c1].bitcast(FP8X4), draft_s)
             nc.vector.tensor_copy(b[:, c0:c1], bank[:])
 
-        w = keep.tile([P, SLOTS], F32, name="w")
-        nc.scalar.activation(w[:], a[:].indirect(list1[:]), COPY, scale=sa_t[:])
-
-        f1 = [keep.tile([P, TOK], F32, name="f1_0"), keep.tile([P, TOK], F32, name="f1_1", tag="a_f1")]
-        nc.vector.memset(f1[0][:], 0.0)
-        nc.gpsimd.memset(f1[1][:], 0.0)
-
         halves = [(h, slice(h * HALF, (h + 1) * HALF), slice(h * HALF // 16, (h + 1) * HALF // 16)) for h in range(2)]
-        v = keep.tile([P, SLOTS], F32, name="v", tag="v_f2")
+        (h0, slots0, cols0), (h1, slots1, cols1) = halves
+        w = keep.tile([P, SLOTS], F32, name="w")
+        for h, slots, cols in halves:
+            nc.scalar.activation(w[:, slots], a[:].indirect(list1[:, cols]), COPY, scale=sa_t[:])
+        f2 = keep.tile([P, TOK], F32, name="f2")
+        nc.vector.memset(f2[:], 0.0)
+        nc.scalar.activation(f2[:].indirect(list4[:, cols0]), w[:, slots0], COPY)
+        f1 = [keep.tile([P, TOK], F32, name="f1_0", tag="cw_f1", align_bytes=64),
+              keep.tile([P, TOK], F32, name="f1_1", tag="a_f1")]
+        for h in range(2):
+            nc.gpsimd.memset(f1[h][:], 0.0)
+
+        v = keep.tile([P, SLOTS], F32, name="v", tag="v_w")
         r = [keep.tile([P, HALF], F32, name="r%d" % h) for h in range(2)]
         for h, slots, cols in halves:
             nc.scalar.activation(v[:, slots], b[:].indirect(list2[:, cols]), COPY, scale=sb_t[:])
             nc.vector.tensor_tensor(r[h][:], w[:, slots], v[:, slots], SUB)
         for h, slots, cols in halves:
             nc.scalar.activation(f1[h][:].indirect(list3[:, cols]), r[h][:], COPY)
-        f2 = keep.tile([P, TOK], F32, name="f2", tag="v_f2")
-        nc.gpsimd.memset(f2[:], 0.0)
-        nc.scalar.activation(f2[:].indirect(list4[:]), w[:], COPY)
+        w_rest = keep.tile([P, HALF], F32, name="w_rest", tag="v_w")
+        nc.vector.tensor_copy(w_rest[:], w[:, slots1])
+        nc.scalar.activation(f2[:].indirect(list4[:, cols1]), w_rest[:], COPY)
 
-        part = keep.tile([P, TOK], F32, name="part")
+        part = keep.tile([P, TOK], F32, name="part", tag="part_bb")
         for n, c0 in enumerate(range(0, TOK, BANK)):
             c1 = c0 + BANK
             bank = scores("c%d" % n, "a%d" % n, c0, c1, arch_w[:, 2 * c0:2 * c1].bitcast(FP4X4), arch_s)
             nc.vector.tensor_tensor(part[:, c0:c1], bank[:], f1[0][:, c0:c1], SUB)
-        cc = keep.tile([P, TOK], F32, name="cc", tag="cc_bb")
+        cc = keep.tile([P, TOK], F32, name="cc")
         nc.vector.tensor_tensor(cc[:], part[:], f1[1][:], SUB)
         left = keep.tile([P, SLOTS], F32, name="left")
-        nc.vector.tensor_copy(left[:], cc[:].indirect(list6[:]))
+        for h, slots, cols in halves:
+            nc.scalar.activation(left[:, slots], cc[:].indirect(list6[:, cols]), COPY)
 
-        bb = keep.tile([P, TOK], F32, name="bb", tag="cc_bb")
+        bb = keep.tile([P, TOK], F32, name="bb", tag="part_bb")
         nc.vector.tensor_tensor(bb[:], b[:], f2[:], MAX)
         y = [keep.tile([P, HALF], F32, name="y%d" % h) for h in range(2)]
         picked = keep.tile([P, HALF], F32, name="picked")
-        (h0, slots0, cols0), (h1, slots1, cols1) = halves
         nc.scalar.activation(picked[:], bb[:].indirect(list5[:, cols1]), COPY)
         nc.vector.tensor_tensor(y[0][:], bb[:].indirect(list5[:, cols0]), left[:, slots0], SUB)
         nc.sync.dma_start(out[:, slots0], y[0][:])

@@ -152,5 +152,8 @@ def tile_attend_scaledlead_three_kernel(tc, query, cache_words, cache_scales, dr
         nc.scalar.activation(picked[:], bb[:].indirect(list5[:, cols1]), COPY)
         nc.vector.tensor_tensor(y[0][:], bb[:].indirect(list5[:, cols0]), left[:, slots0], SUB)
         nc.sync.dma_start(out[:, slots0], y[0][:])
-        nc.vector.tensor_tensor(y[1][:], picked[:], left[:, slots1], SUB)
-        nc.scalar.dma_start(out[:, slots1], y[1][:])
+        for queue, s0 in ((nc.sync, 0), (nc.scalar, HALF // 2)):
+            piece = slice(s0, s0 + HALF // 2)
+            slots = slice(HALF + s0, HALF + s0 + HALF // 2)
+            nc.vector.tensor_tensor(y[1][:, piece], picked[:, piece], left[:, slots], SUB)
+            queue.dma_start(out[:, slots], y[1][:, piece])

@@ -151,7 +151,9 @@ def tile_attend_scaledlead_three_kernel(tc, query, cache_words, cache_scales, dr
         picked = keep.tile([P, HALF], F32, name="picked")
         nc.scalar.activation(picked[:], bb[:].indirect(list5[:, cols1]), COPY)
         nc.vector.tensor_tensor(y[0][:], bb[:].indirect(list5[:, cols0]), left[:, slots0], SUB)
-        nc.sync.dma_start(out[:, slots0], y[0][:])
+        for queue, s0 in ((nc.sync, 0), (nc.scalar, HALF // 2)):
+            piece = slice(s0, s0 + HALF // 2)
+            queue.dma_start(out[:, piece], y[0][:, piece])
         for queue, s0 in ((nc.sync, 0), (nc.scalar, HALF // 2)):
             piece = slice(s0, s0 + HALF // 2)
             slots = slice(HALF + s0, HALF + s0 + HALF // 2)

from contextlib import ExitStack

import concourse.mybir as mybir

F32 = mybir.dt.float32
BF16 = mybir.dt.bfloat16
I32 = mybir.dt.int32
U32 = mybir.dt.uint32
U16 = mybir.dt.uint16
U8 = mybir.dt.uint8
FP8X4 = mybir.dt.float8_e4m3fn_x4
FP4X4 = mybir.dt.float4_e2m1fn_x4
COPY = mybir.ActivationFunctionType.Copy
SUB = mybir.AluOpType.subtract
MAX = mybir.AluOpType.max

P = 128
PACK = 4
Q = 128
TOK = 1024
SLOTS = 512
HALF = SLOTS // 2
BANK = 512
FLOPS = 3 * 2 * 512 * Q * TOK


def tile_attend_scaledlead_three_kernel(tc, query, cache_words, cache_scales, draft_words, draft_scales,
                                         arch_words, arch_scales, sa, sb, offs, offs2, offs3, offs4, offs5,
                                         offs6, out):
    nc = tc.nc
    with ExitStack() as ctx:
        keep = ctx.enter_context(tc.tile_pool(name="keep", bufs=1))
        psum = ctx.enter_context(tc.psum_pool(name="psum", bufs=1))

        def load_list(src, name):
            t = keep.tile([P, SLOTS // 16], U16, name=name)
            nc.sync.dma_start(t[:], src)
            return t

        def plane(name):
            t = keep.tile([P, TOK], U8, name=name, align_bytes=64)
            nc.vector.memset(t[:].bitcast(I32), 0)
            return t

        def load_scales(queue, t, src, g):
            queue.dma_start(t[32 * g:32 * g + 4, :].bitcast(I32), src[0, 4 * g:4 * g + 4, :].bitcast(I32))

        cache_s = plane("cache_s")
        draft_s = plane("draft_s")
        arch_s = plane("arch_s")
        q_raw = keep.tile([P, PACK, Q], F32, name="q_raw")
        cache_w = keep.tile([P, 2 * TOK], U8, name="cache_w", tag="cw_f1", align_bytes=64)
        draft_w = keep.tile([P, TOK], I32, name="draft_w", align_bytes=64)
        arch_w = keep.tile([P, 2 * TOK], U8, name="arch_w", align_bytes=64)
        sa_t = keep.tile([P, 1], F32, name="sa_t")
        sb_t = keep.tile([P, 1], F32, name="sb_t")
        nc.sync.dma_start(q_raw[:], query.rearrange("(p j) q -> p j q", j=PACK))
        nc.sync.dma_start(cache_w[:].bitcast(I32), cache_words[0].bitcast(I32))
        load_scales(nc.sync, cache_s, cache_scales, 0)
        load_scales(nc.sync, cache_s, cache_scales, 1)
        load_scales(nc.sync, cache_s, cache_scales, 2)
        load_scales(nc.sync, cache_s, cache_scales, 3)
        nc.sync.dma_start(sa_t[:], sa)
        nc.sync.dma_start(draft_w[:], draft_words[0].rearrange("p n t -> p (n t)").bitcast(I32))
        list1 = load_list(offs, "list1")
        load_scales(nc.sync, draft_s, draft_scales, 0)
        load_scales(nc.sync, draft_s, draft_scales, 1)
        load_scales(nc.sync, draft_s, draft_scales, 2)
        load_scales(nc.sync, draft_s, draft_scales, 3)
        list4 = load_list(offs4, "list4")
        list2 = load_list(offs2, "list2")
        nc.sync.dma_start(sb_t[:], sb)
        list3 = load_list(offs3, "list3")
        nc.sync.dma_start(arch_w[:].bitcast(I32), arch_words[0].bitcast(I32))
        load_scales(nc.sync, arch_s, arch_scales, 0)
        load_scales(nc.sync, arch_s, arch_scales, 1)
        load_scales(nc.sync, arch_s, arch_scales, 2)
        load_scales(nc.sync, arch_s, arch_scales, 3)
        list6 = load_list(offs6, "list6")
        list5 = load_list(offs5, "list5")

        q_bf = keep.tile([P, Q, PACK], BF16, name="q_bf", align_bytes=64)
        q_w = keep.tile([P, Q], U32, name="q_w", align_bytes=64)
        q_s = keep.tile([P, Q], U8, name="q_s", align_bytes=64)
        q_halves = [slice(0, Q // 2), slice(Q // 2, Q)]
        for qs in q_halves:
            nc.vector.tensor_copy(q_bf[:, qs, :].rearrange("p (c i) t -> p c t i", i=4),
                                  q_raw[:, :, qs].rearrange("p t (c i) -> p c t i", i=4))
        for qs in q_halves:
            nc.vector.quantize_mx(out=q_w[:, qs].bitcast(FP8X4), scales=q_s[:, qs],
                                  in_=q_bf[:, qs, :].rearrange("p c t -> p (c t)"))

        def scores(name, tag, c0, c1, rhs, rhs_scale):
            bank = psum.tile([P, c1 - c0], F32, name=name, tag=tag)
            nc.tensor.matmul_mx(out=bank[:], lhsT=q_w[:].bitcast(FP8X4), lhsT_scale=q_s[:],
                                rhs=rhs, rhs_scale=rhs_scale[:, c0:c1], start=True, stop=True)
            return bank

        a = keep.tile([P, TOK], F32, name="a", tag="a_f1")
        for n, (c0, c1) in enumerate(((0, 512), (512, 768), (768, 896), (896, 1024))):
            bank = scores("a%d" % n, "a%d" % n, c0, c1, cache_w[:, 2 * c0:2 * c1].bitcast(FP4X4), cache_s)
            if n % 2 == 0:
                nc.scalar.copy(a[:, c0:c1], bank[:])
            else:
                nc.vector.tensor_copy(a[:, c0:c1], bank[:])

        b = keep.tile([P, TOK], F32, name="b")
        for n, c0 in enumerate(range(0, TOK, 256)):
            c1 = c0 + 256
            bank = scores("b%d" % n, "b%d" % n, c0, c1, draft_w[:, c0:c1].bitcast(FP8X4), draft_s)
            nc.vector.tensor_copy(b[:, c0:c1], bank[:])

        halves = [(h, slice(h * HALF, (h + 1) * HALF), slice(h * HALF // 16, (h + 1) * HALF // 16)) for h in range(2)]
        (h0, slots0, cols0), (h1, slots1, cols1) = halves
        w = keep.tile([P, SLOTS], F32, name="w")
        for h, slots, cols in halves:
            nc.scalar.activation(w[:, slots], a[:].indirect(list1[:, cols]), COPY, scale=sa_t[:])
        f2 = keep.tile([P, TOK], F32, name="f2")
        nc.vector.memset(f2[:], 0.0)
        nc.scalar.activation(f2[:].indirect(list4[:, cols0]), w[:, slots0], COPY)
        f1 = [keep.tile([P, TOK], F32, name="f1_0", tag="cw_f1", align_bytes=64),
              keep.tile([P, TOK], F32, name="f1_1", tag="a_f1")]
        for h in range(2):
            nc.gpsimd.memset(f1[h][:], 0.0)

        v = keep.tile([P, SLOTS], F32, name="v", tag="v_w")
        r = [keep.tile([P, HALF], F32, name="r%d" % h) for h in range(2)]
        for h, slots, cols in halves:
            nc.scalar.activation(v[:, slots], b[:].indirect(list2[:, cols]), COPY, scale=sb_t[:])
            nc.vector.tensor_tensor(r[h][:], w[:, slots], v[:, slots], SUB)
        for h, slots, cols in halves:
            nc.scalar.activation(f1[h][:].indirect(list3[:, cols]), r[h][:], COPY)
        w_rest = keep.tile([P, HALF], F32, name="w_rest", tag="v_w")
        nc.vector.tensor_copy(w_rest[:], w[:, slots1])
        nc.scalar.activation(f2[:].indirect(list4[:, cols1]), w_rest[:], COPY)

        part = keep.tile([P, TOK], F32, name="part", tag="part_bb")
        for n, c0 in enumerate(range(0, TOK, BANK)):
            c1 = c0 + BANK
            bank = scores("c%d" % n, "a%d" % n, c0, c1, arch_w[:, 2 * c0:2 * c1].bitcast(FP4X4), arch_s)
            nc.vector.tensor_tensor(part[:, c0:c1], bank[:], f1[0][:, c0:c1], SUB)
        cc = keep.tile([P, TOK], F32, name="cc")
        nc.vector.tensor_tensor(cc[:], part[:], f1[1][:], SUB)
        left = keep.tile([P, SLOTS], F32, name="left")
        for h, slots, cols in halves:
            nc.scalar.activation(left[:, slots], cc[:].indirect(list6[:, cols]), COPY)

        bb = keep.tile([P, TOK], F32, name="bb", tag="part_bb")
        nc.vector.tensor_tensor(bb[:], b[:], f2[:], MAX)
        y = [keep.tile([P, HALF], F32, name="y%d" % h) for h in range(2)]
        picked = keep.tile([P, HALF], F32, name="picked")
        nc.scalar.activation(picked[:], bb[:].indirect(list5[:, cols1]), COPY)
        nc.vector.tensor_tensor(y[0][:], bb[:].indirect(list5[:, cols0]), left[:, slots0], SUB)
        for queue, s0 in ((nc.sync, 0), (nc.scalar, HALF // 2)):
            piece = slice(s0, s0 + HALF // 2)
            queue.dma_start(out[:, piece], y[0][:, piece])
        for queue, s0 in ((nc.sync, 0), (nc.scalar, HALF // 2)):
            piece = slice(s0, s0 + HALF // 2)
            slots = slice(HALF + s0, HALF + s0 + HALF // 2)
            nc.vector.tensor_tensor(y[1][:, piece], picked[:, piece], left[:, slots], SUB)
            queue.dma_start(out[:, slots], y[1][:, piece])
